import numpy as np
import ml_dtypes


def mxq(x, axis, fmt="e4m3"):
    dtype, down = {"e4m3": (ml_dtypes.float8_e4m3fn, 7), "e5m2": (ml_dtypes.float8_e5m2, 14)}[fmt]
    v = np.moveaxis(np.asarray(x, np.float32).astype(ml_dtypes.bfloat16).astype(np.float64), axis, -1)
    blocks = v.reshape(v.shape[:-1] + (-1, 32))
    amax = np.abs(blocks).max(-1, keepdims=True)
    byte = np.maximum(np.where(amax > 0, np.frexp(amax)[1] - 1 + 127, 0) - down, 1)
    scale = np.exp2(byte - 127.0)
    codes = (blocks / scale).astype(np.float32).astype(dtype).astype(np.float64)
    return np.moveaxis((codes * scale).reshape(v.shape), -1, axis)


WIDE = False


def mx_kscale(k):
    if not WIDE:
        return np.ones(k)
    levels = np.array([10, -10, 5, -5, 0])
    if k % 512:
        return np.exp2(np.random.permutation(np.resize(levels, k // 32))).repeat(32)
    a = np.empty((k // 512, 16))
    for p in range(k // 512):
        a[p, :8] = np.random.permutation(np.resize(levels, 8))
        for g in range(8):
            far = levels[np.abs(levels - a[p, g]) >= 10]
            a[p, g + 8] = far[np.random.randint(len(far))]
    return np.exp2(a.ravel()).repeat(32)


def f64(x):
    return np.asarray(x).astype(np.float64)


def striped(idx):
    return np.tile(idx.reshape(-1, 16).T, (8, 1)).astype(np.uint16)


def unstriped(offs):
    return offs[:16].T.reshape(-1).astype(np.int64)


E2M1 = np.array([0.0, 0.5, 1.0, 1.5, 2.0, 3.0, 4.0, 6.0, -0.0, -0.5, -1.0, -1.5, -2.0, -3.0, -4.0, -6.0])


def pack_weight(w, fmt):
    k, n = w.shape
    w = f64(np.asarray(w, np.float32).astype(ml_dtypes.bfloat16)).reshape(k // 32, 32, n)
    amax = np.abs(w).max(1)
    if fmt == "e4m3":
        byte = np.frexp(amax)[1] - 1 + 127 - 7
    else:
        mant, ex = np.frexp(amax / 6.0)
        byte = np.where(mant > 0.5, ex, ex - 1) + 127
    byte = np.clip(np.where(amax > 0, byte, 1), 1, 254)
    scaled = (w * np.exp2(127.0 - byte)[:, None, :]).reshape(k, n).astype(np.float32)
    by_word = np.ascontiguousarray(scaled.reshape(k // 512, 128, 4, n).transpose(0, 1, 3, 2))
    if fmt == "e4m3":
        words = by_word.astype(ml_dtypes.float8_e4m3fn).view(np.uint8)
    else:
        c = by_word.astype(ml_dtypes.float4_e2m1fn).view(np.uint8) & 0xF
        words = (c[..., 0::2] | (c[..., 1::2] << 4)).reshape(k // 512, 128, 2 * n)
    return np.ascontiguousarray(words), np.ascontiguousarray(byte.astype(np.uint8).reshape(k // 512, 16, n))


def unpack_weight(words, scales, fmt):
    g, _, n = scales.shape
    words = np.ascontiguousarray(words).reshape(g, 128, n, -1)
    if fmt == "e4m3":
        vals = words.view(ml_dtypes.float8_e4m3fn).astype(np.float64)
    else:
        nib = np.empty((g, 128, n, 4), np.uint8)
        nib[..., 0::2] = words & 0xF
        nib[..., 1::2] = words >> 4
        vals = E2M1[nib]
    vals = vals * np.repeat(np.exp2(scales.astype(np.float64) - 127.0), 8, axis=1)[..., None]
    return vals.transpose(0, 1, 3, 2).reshape(g * 512, n)


def gelu(v):
    return 0.5 * v * (1.0 + np.tanh(np.sqrt(2.0 / np.pi) * (v + 0.044715 * v**3)))


K, K1, T, S, S2 = 1024, 512, 2048, 1024, 512


def setup_inputs():
    n = np.random.standard_normal
    s = mx_kscale(K)[:, None]
    d = {}
    d["tab_words"], d["tab_scales"] = pack_weight(n((K, T)) * s, "e4m3")
    d["offs"] = striped(np.random.permutation(T)[:S])
    d["offs2"] = striped(np.random.permutation(T)[:S2])
    d["wcut"] = (n((K1, K)) / K / s[:K1] / s.T).astype(np.float32)
    d["wway_words"], d["wway_scales"] = pack_weight(n((K - K1, K)) / K / s[K1:] / s.T, "e2m1")
    d["base"] = (0.8 * n((S2, S)) + 0.3).astype(np.float32)
    d["tol"] = (0.8 * n(S2) - 0.3).astype(np.float32)
    return d


def reference(tab_words, tab_scales, offs, offs2, wcut, wway_words, wway_scales, base, tol):
    TW = unpack_weight(tab_words, tab_scales, "e4m3")
    v = TW[:, unstriped(offs)]
    v2 = TW[:, unstriped(offs2)]
    wc = mxq(f64(wcut), 0, "e4m3")
    ww = unpack_weight(wway_words, wway_scales, "e2m1")
    h = np.abs(wc.T @ v[:K1] + ww.T @ v[K1:])
    hq = mxq(h, 0, "e4m3")
    e = v2.T @ hq
    upper = np.maximum(e, f64(base))
    lower = np.minimum(e, f64(tol)[:, None])
    return upper - lower

@@ -1,0 +1,151 @@
+from contextlib import ExitStack
+
+import concourse.mybir as mybir
+
+F32 = mybir.dt.float32
+BF16 = mybir.dt.bfloat16
+I32 = mybir.dt.int32
+U32 = mybir.dt.uint32
+U16 = mybir.dt.uint16
+U8 = mybir.dt.uint8
+E4M3 = mybir.dt.float8_e4m3fn_x4
+E2M1 = mybir.dt.float4_e2m1fn_x4
+ALU = mybir.AluOpType
+ACT = mybir.ActivationFunctionType
+
+P = 128
+K, T, S, S2 = 1024, 2048, 1024, 512
+FLOPS = 2 * K * K * S + 2 * K * S2 * S
+
+
+def tile_list_keying_risk_scores_kernel(tc, tab_words, tab_scales, offs, offs2, wcut, wway_words, wway_scales, base, tol, out):
+    nc = tc.nc
+    with ExitStack() as ctx:
+        keep = ctx.enter_context(tc.tile_pool(name="keep", bufs=1))
+        ring = ctx.enter_context(tc.tile_pool(name="ring", bufs=4))
+        ps = ctx.enter_context(tc.psum_pool(name="ps", bufs=8))
+
+        keys = keep.tile([P, S // 16], U16, name="keys")
+        cyls = keep.tile([P, S2 // 16], U16, name="cyls")
+        ts = keep.tile([P, T // 4], I32, name="ts", align_bytes=64)
+        ws = keep.tile([P, K // 4], I32, name="ws", align_bytes=64)
+        ww = keep.tile([P, K // 2], I32, name="ww", align_bytes=64)
+        tw = [keep.tile([P, T], I32, name="tw%d" % a, align_bytes=64) for a in range(2)]
+        wc = [keep.tile([P, 4, 512], F32, name="wc%d" % b, align_bytes=64) for b in range(2)]
+        bs = [keep.tile([P, 4, 512], F32, name="bs%d" % h, align_bytes=64) for h in range(2)]
+        tl = keep.tile([P, 4], F32, name="tl")
+
+        nc.vector.memset(ws[:], 0)
+        nc.vector.memset(ts[:], 0)
+        nc.sync.dma_start(ww[:], wway_words[0].bitcast(I32))
+        for q in range(4):
+            eng = nc.sync if q % 2 else nc.scalar
+            eng.dma_start(ws[32 * q:32 * q + 4, :], wway_scales[0, 4 * q:4 * q + 4, :].bitcast(I32))
+        for a in (1, 0):
+            for q in range(4):
+                r0 = 32 * q + 4 * (1 - a)
+                eng = nc.sync if q % 2 else nc.scalar
+                eng.dma_start(ts[r0:r0 + 4, :], tab_scales[a, 4 * q:4 * q + 4, :].bitcast(I32))
+        nc.sync.dma_start(keys[:], offs)
+        nc.sync.dma_start(cyls[:], offs2)
+        nc.sync.dma_start(wc[0][:], wcut[:, 0:512].rearrange("(p j) c -> p j c", j=4))
+        nc.sync.dma_start(tw[1][:], tab_words[1].rearrange("p t i -> p (t i)").bitcast(I32))
+        nc.sync.dma_start(wc[1][:], wcut[:, 512:1024].rearrange("(p j) c -> p j c", j=4))
+        nc.sync.dma_start(tw[0][:], tab_words[0].rearrange("p t i -> p (t i)").bitcast(I32))
+        with nc.allow_non_contiguous_dma(reason="one tolerance a partition"):
+            nc.sync.dma_start(tl[:], tol.rearrange("(i p) -> p i", p=P))
+        for h in range(2):
+            nc.sync.dma_start(bs[h][:], base[:, 512 * h:512 * h + 512].rearrange("(i p) j -> p i j", p=P))
+
+        kw = [keep.tile([P, S], U32, name="kw%d" % a, align_bytes=64) for a in range(2)]
+        ks = keep.tile([P, S], U8, name="ks", align_bytes=64)
+        cw = [keep.tile([P, S2], U32, name="cw%d" % a, align_bytes=64) for a in range(2)]
+        cs = keep.tile([P, S2], U8, name="cs", align_bytes=64)
+        wwp = keep.tile([P, 2 * K], U8, name="wwp", align_bytes=64)
+        wsp = keep.tile([P, K], U8, name="wsp", align_bytes=64)
+        wcb = [keep.tile([P, 2048], BF16, name="wcb%d" % b, tag="wcb%d" % b, align_bytes=64) for b in range(2)]
+        wcq = [keep.tile([P, 512], U32, name="wcq%d" % b, align_bytes=64) for b in range(2)]
+        wcs = [keep.tile([P, 512], U8, name="wcs%d" % b, align_bytes=64) for b in range(2)]
+        hq = [keep.tile([P, S], U32, name="hq%d" % b, align_bytes=64) for b in range(2)]
+        hs = [keep.tile([P, S], U8, name="hs%d" % b, align_bytes=64) for b in range(2)]
+
+        def gather_scales(dst, lst, j0, j1):
+            nc.vector.tensor_copy(dst[:, j0:j1], ts[:].bitcast(U8).indirect(lst[:, j0 // 16:j1 // 16]))
+
+        def gather_words(dst, a, lst, j0, j1):
+            nc.vector.tensor_copy(dst[a][:, j0:j1], tw[a][:].bitcast(U32).indirect(lst[:, j0 // 16:j1 // 16]))
+
+        def cast(b):
+            nc.scalar.activation(
+                wcb[b][:].rearrange("p (t m j) -> p m j t", t=4, j=4),
+                wc[b][:].rearrange("p j (m t) -> p m j t", t=4), ACT.Copy)
+
+        def quant_w(b):
+            nc.vector.quantize_mx(wcq[b][:].bitcast(E4M3), wcs[b][:], wcb[b][:])
+
+        def stage1(b, j0):
+            hb = ring.tile([P, 256, 4], BF16, name="hb", align_bytes=64, bufs=8)
+            for c in range(2):
+                n = slice(j0 + 128 * c, j0 + 128 * c + 128)
+                acc = ps.tile([P, 4, 128], F32, name="acc")
+                for t in range(4):
+                    c0 = 512 * b + 128 * t
+                    nc.tensor.matmul_mx(acc[:, t, :], lhsT=wwp[:, 2 * c0:2 * c0 + 256].bitcast(E2M1), lhsT_scale=wsp[:, c0:c0 + 128],
+                                        rhs=kw[1][:, n].bitcast(E4M3), rhs_scale=ks[:, n], start=(t == 0), stop=False)
+                for t in range(4):
+                    nc.tensor.matmul_mx(acc[:, t, :], lhsT=wcq[b][:, 128 * t:128 * t + 128].bitcast(E4M3), lhsT_scale=wcs[b][:, 128 * t:128 * t + 128],
+                                        rhs=kw[0][:, n].bitcast(E4M3), rhs_scale=ks[4:P, n], start=False, stop=(t == 3))
+                nc.scalar.activation(hb[:, 128 * c:128 * c + 128, :], acc[:].rearrange("p t n -> p n t"), ACT.Abs)
+            nc.vector.quantize_mx(hq[b][:, j0:j0 + 256].bitcast(E4M3), hs[b][:, j0:j0 + 256], hb[:].rearrange("p n t -> p (n t)"))
+
+        def stage2(j0):
+            h, o = divmod(j0, 512)
+            n = slice(j0, j0 + 256)
+            tiles = []
+            for pair in range(2):
+                acc = ps.tile([P, 2, 256], F32, name="acc")
+                for u in range(2):
+                    m = slice(256 * pair + 128 * u, 256 * pair + 128 * u + 128)
+                    nc.tensor.matmul_mx(acc[:, u, :], lhsT=cw[0][:, m].bitcast(E4M3), lhsT_scale=cs[4:P, m],
+                                        rhs=hq[0][:, n].bitcast(E4M3), rhs_scale=hs[0][:, n], start=True, stop=False)
+                    nc.tensor.matmul_mx(acc[:, u, :], lhsT=cw[1][:, m].bitcast(E4M3), lhsT_scale=cs[:, m],
+                                        rhs=hq[1][:, n].bitcast(E4M3), rhs_scale=hs[1][:, n], start=False, stop=True)
+                up = ring.tile([P, 2, 256], F32, name="up")
+                nc.vector.tensor_tensor(up[:], acc[:], bs[h][:, 2 * pair:2 * pair + 2, o:o + 256], ALU.max)
+                tiles.append((pair, acc, up))
+            for pair, acc, up in tiles:
+                res = ring.tile([P, 2, 256], F32, name="res", bufs=8)
+                for u in range(2):
+                    i = 2 * pair + u
+                    nc.vector.scalar_tensor_tensor(res[:, u, :], acc[:, u, :], tl[:, i:i + 1], up[:, u, :], ALU.min, ALU.subtract, reverse1=True)
+                nc.sync.dma_start(out[256 * pair:256 * pair + 256, n].rearrange("(u p) j -> p u j", p=P), res[:])
+
+        nc.vector.tensor_copy(wsp[:].rearrange("p (b t m) -> p b m t", b=2, t=4),
+                              ws[:].bitcast(U8).rearrange("p (b m t) -> p b m t", b=2, t=4))
+        nc.vector.tensor_copy(wwp[:].bitcast(U16).rearrange("p (b t m) -> p b m t", b=2, t=4),
+                              ww[:].bitcast(U16).rearrange("p (b m t) -> p b m t", b=2, t=4))
+        gather_scales(ks, keys, 0, 1024)
+        gather_scales(cs, cyls, 0, 512)
+        gather_words(kw, 1, keys, 0, 512)
+        gather_words(kw, 1, keys, 512, 1024)
+        cast(0)
+        quant_w(0)
+        gather_words(cw, 1, cyls, 0, 512)
+        cast(1)
+        gather_words(kw, 0, keys, 0, 256)
+        quant_w(1)
+        gather_words(kw, 0, keys, 256, 512)
+        stage1(0, 0)
+        stage1(1, 0)
+        gather_words(cw, 0, cyls, 0, 512)
+        gather_words(kw, 0, keys, 512, 1024)
+        stage1(0, 256)
+        stage1(1, 256)
+        stage2(0)
+        stage1(0, 512)
+        stage1(1, 512)
+        stage2(256)
+        stage1(0, 768)
+        stage1(1, 768)
+        stage2(512)
+        stage2(768)

@@ -41,15 +41,16 @@ def tile_list_keying_risk_scores_kernel(tc, tab_words, tab_scales, offs, offs2, 
         for q in range(4):
             eng = nc.sync if q % 2 else nc.scalar
             eng.dma_start(ws[32 * q:32 * q + 4, :], wway_scales[0, 4 * q:4 * q + 4, :].bitcast(I32))
+        nc.sync.dma_start(tw[1][:], tab_words[1].rearrange("p t i -> p (t i)").bitcast(I32))
         for a in (1, 0):
             for q in range(4):
                 r0 = 32 * q + 4 * (1 - a)
-                eng = nc.sync if q % 2 else nc.scalar
+                if (a, q) == (0, 3):
+                    nc.sync.dma_start(keys[:], offs)
+                eng = nc.sync if (a, q) == (0, 3) else nc.scalar
                 eng.dma_start(ts[r0:r0 + 4, :], tab_scales[a, 4 * q:4 * q + 4, :].bitcast(I32))
-        nc.sync.dma_start(keys[:], offs)
-        nc.sync.dma_start(cyls[:], offs2)
         nc.sync.dma_start(wc[0][:], wcut[:, 0:512].rearrange("(p j) c -> p j c", j=4))
-        nc.sync.dma_start(tw[1][:], tab_words[1].rearrange("p t i -> p (t i)").bitcast(I32))
+        nc.sync.dma_start(cyls[:], offs2)
         nc.sync.dma_start(wc[1][:], wcut[:, 512:1024].rearrange("(p j) c -> p j c", j=4))
         nc.sync.dma_start(tw[0][:], tab_words[0].rearrange("p t i -> p (t i)").bitcast(I32))
         with nc.allow_non_contiguous_dma(reason="one tolerance a partition"):
@@ -57,9 +58,10 @@ def tile_list_keying_risk_scores_kernel(tc, tab_words, tab_scales, offs, offs2, 
         for h in range(2):
             nc.sync.dma_start(bs[h][:], base[:, 512 * h:512 * h + 512].rearrange("(i p) j -> p i j", p=P))
 
-        kw = [keep.tile([P, S], U32, name="kw%d" % a, align_bytes=64) for a in range(2)]
+        kw1 = keep.tile([P, S], U32, name="kw1", align_bytes=64)
+        kw0 = {}
         ks = keep.tile([P, S], U8, name="ks", align_bytes=64)
-        cw = [keep.tile([P, S2], U32, name="cw%d" % a, align_bytes=64) for a in range(2)]
+        cw = {}
         cs = keep.tile([P, S2], U8, name="cs", align_bytes=64)
         wwp = keep.tile([P, 2 * K], U8, name="wwp", align_bytes=64)
         wsp = keep.tile([P, K], U8, name="wsp", align_bytes=64)
@@ -73,32 +75,32 @@ def tile_list_keying_risk_scores_kernel(tc, tab_words, tab_scales, offs, offs2, 
             nc.vector.tensor_copy(dst[:, j0:j1], ts[:].bitcast(U8).indirect(lst[:, j0 // 16:j1 // 16]))
 
         def gather_words(dst, a, lst, j0, j1):
-            nc.vector.tensor_copy(dst[a][:, j0:j1], tw[a][:].bitcast(U32).indirect(lst[:, j0 // 16:j1 // 16]))
+            nc.vector.tensor_copy(dst, tw[a][:].bitcast(U32).indirect(lst[:, j0 // 16:j1 // 16]))
 
         def cast(b):
             nc.scalar.activation(
-                wcb[b][:].rearrange("p (t m j) -> p m j t", t=4, j=4),
-                wc[b][:].rearrange("p j (m t) -> p m j t", t=4), ACT.Copy)
+                wcb[b][:].rearrange("p (t m j) -> p m t j", t=4, j=4),
+                wc[b][:].rearrange("p j (m t) -> p m t j", t=4), ACT.Copy)
 
         def quant_w(b):
             nc.vector.quantize_mx(wcq[b][:].bitcast(E4M3), wcs[b][:], wcb[b][:])
 
         def stage1(b, j0):
-            hb = ring.tile([P, 256, 4], BF16, name="hb", align_bytes=64, bufs=8)
+            hb = keep.tile([P, 256, 4], BF16, name="hb", tag="hb%d_%d" % (b, j0), align_bytes=64)
             for c in range(2):
                 n = slice(j0 + 128 * c, j0 + 128 * c + 128)
                 acc = ps.tile([P, 4, 128], F32, name="acc")
                 for t in range(4):
                     c0 = 512 * b + 128 * t
                     nc.tensor.matmul_mx(acc[:, t, :], lhsT=wwp[:, 2 * c0:2 * c0 + 256].bitcast(E2M1), lhsT_scale=wsp[:, c0:c0 + 128],
-                                        rhs=kw[1][:, n].bitcast(E4M3), rhs_scale=ks[:, n], start=(t == 0), stop=False)
+                                        rhs=kw1[:, n].bitcast(E4M3), rhs_scale=ks[:, n], start=(t == 0), stop=False)
                 for t in range(4):
                     nc.tensor.matmul_mx(acc[:, t, :], lhsT=wcq[b][:, 128 * t:128 * t + 128].bitcast(E4M3), lhsT_scale=wcs[b][:, 128 * t:128 * t + 128],
-                                        rhs=kw[0][:, n].bitcast(E4M3), rhs_scale=ks[4:P, n], start=False, stop=(t == 3))
+                                        rhs=kw0[j0 // 512][:, n.start % 512:n.start % 512 + 128].bitcast(E4M3), rhs_scale=ks[4:P, n], start=False, stop=(t == 3))
                 nc.scalar.activation(hb[:, 128 * c:128 * c + 128, :], acc[:].rearrange("p t n -> p n t"), ACT.Abs)
             nc.vector.quantize_mx(hq[b][:, j0:j0 + 256].bitcast(E4M3), hs[b][:, j0:j0 + 256], hb[:].rearrange("p n t -> p (n t)"))
 
-        def stage2(j0):
+        def stage2(j0, shared):
             h, o = divmod(j0, 512)
             n = slice(j0, j0 + 256)
             tiles = []
@@ -111,41 +113,57 @@ def tile_list_keying_risk_scores_kernel(tc, tab_words, tab_scales, offs, offs2, 
                     nc.tensor.matmul_mx(acc[:, u, :], lhsT=cw[1][:, m].bitcast(E4M3), lhsT_scale=cs[:, m],
                                         rhs=hq[1][:, n].bitcast(E4M3), rhs_scale=hs[1][:, n], start=False, stop=True)
                 up = ring.tile([P, 2, 256], F32, name="up")
-                nc.vector.tensor_tensor(up[:], acc[:], bs[h][:, 2 * pair:2 * pair + 2, o:o + 256], ALU.max)
+                if pair < shared:
+                    nc.vector.tensor_tensor(up[:], bs[h][:, 2 * pair:2 * pair + 2, o:o + 256], acc[:], ALU.subtract)
+                else:
+                    nc.vector.tensor_tensor(up[:], acc[:], bs[h][:, 2 * pair:2 * pair + 2, o:o + 256], ALU.max)
                 tiles.append((pair, acc, up))
             for pair, acc, up in tiles:
                 res = ring.tile([P, 2, 256], F32, name="res", bufs=8)
-                for u in range(2):
-                    i = 2 * pair + u
-                    nc.vector.scalar_tensor_tensor(res[:, u, :], acc[:, u, :], tl[:, i:i + 1], up[:, u, :], ALU.min, ALU.subtract, reverse1=True)
+                if pair < shared:
+                    over = ring.tile([P, 2, 256], F32, name="over")
+                    under = ring.tile([P, 2, 256], F32, name="under")
+                    for u in range(2):
+                        i = 2 * pair + u
+                        nc.scalar.activation(over[:, u, :], acc[:, u, :], ACT.Relu, bias=tl[:, i:i + 1])
+                    nc.scalar.activation(under[:], up[:], ACT.Relu)
+                    nc.gpsimd.tensor_tensor(res[:], over[:], under[:], ALU.add)
+                else:
+                    for u in range(2):
+                        i = 2 * pair + u
+                        nc.vector.scalar_tensor_tensor(res[:, u, :], acc[:, u, :], tl[:, i:i + 1], up[:, u, :], ALU.min, ALU.subtract, reverse1=True)
                 nc.sync.dma_start(out[256 * pair:256 * pair + 256, n].rearrange("(u p) j -> p u j", p=P), res[:])
 
-        nc.vector.tensor_copy(wsp[:].rearrange("p (b t m) -> p b m t", b=2, t=4),
-                              ws[:].bitcast(U8).rearrange("p (b m t) -> p b m t", b=2, t=4))
-        nc.vector.tensor_copy(wwp[:].bitcast(U16).rearrange("p (b t m) -> p b m t", b=2, t=4),
-                              ww[:].bitcast(U16).rearrange("p (b m t) -> p b m t", b=2, t=4))
-        gather_scales(ks, keys, 0, 1024)
+        nc.vector.tensor_copy(wsp[:].rearrange("p (b t o i) -> p b o t i", b=2, t=4, i=16),
+                              ws[:].bitcast(U8).rearrange("p (b o i t) -> p b o t i", b=2, t=4, i=16))
+        nc.vector.tensor_copy(wwp[:].bitcast(U16).rearrange("p (b t o i) -> p b o t i", b=2, t=4, i=8),
+                              ww[:].bitcast(U16).rearrange("p (b o i t) -> p b o t i", b=2, t=4, i=8))
+        gather_words(kw1[:], 1, keys, 0, 1024)
+        gather_scales(ks, keys, 0, 512)
+        gather_scales(ks, keys, 512, 1024)
         gather_scales(cs, cyls, 0, 512)
-        gather_words(kw, 1, keys, 0, 512)
-        gather_words(kw, 1, keys, 512, 1024)
         cast(0)
         quant_w(0)
-        gather_words(cw, 1, cyls, 0, 512)
         cast(1)
-        gather_words(kw, 0, keys, 0, 256)
+        kw0[0] = keep.tile([P, 512], U32, name="kw0a", align_bytes=64)
+        gather_words(kw0[0][:, 0:256], 0, keys, 0, 256)
         quant_w(1)
-        gather_words(kw, 0, keys, 256, 512)
+        gather_words(kw0[0][:, 256:512], 0, keys, 256, 512)
+        cw[1] = keep.tile([P, S2], U32, name="cw1", tag="wcb1", align_bytes=64)
+        gather_words(cw[1][:], 1, cyls, 0, 512)
+        cw[0] = keep.tile([P, S2], U32, name="cw0", align_bytes=64)
+        gather_words(cw[0][:], 0, cyls, 0, 512)
         stage1(0, 0)
         stage1(1, 0)
-        gather_words(cw, 0, cyls, 0, 512)
-        gather_words(kw, 0, keys, 512, 1024)
+        kw0[1] = keep.tile([P, 512], U32, name="kw0b", tag="hb1_0", align_bytes=64)
+        gather_words(kw0[1][:], 0, keys, 512, 1024)
         stage1(0, 256)
         stage1(1, 256)
-        stage2(0)
+        stage2(0, 0)
         stage1(0, 512)
         stage1(1, 512)
-        stage2(256)
+        stage2(256, 0)
         stage1(0, 768)
         stage1(1, 768)
-        stage2(512)
-        stage2(768)
+        stage2(512, 0)
+        stage2(768, 0)

@@ -39,17 +39,20 @@ def tile_list_keying_risk_scores_kernel(tc, tab_words, tab_scales, offs, offs2, 
         nc.vector.memset(ts[:], 0)
         nc.sync.dma_start(ww[:], wway_words[0].bitcast(I32))
         for q in range(4):
-            eng = nc.sync if q % 2 else nc.scalar
-            eng.dma_start(ws[32 * q:32 * q + 4, :], wway_scales[0, 4 * q:4 * q + 4, :].bitcast(I32))
+            nc.sync.dma_start(ws[32 * q:32 * q + 4, :], wway_scales[0, 4 * q:4 * q + 4, :].bitcast(I32))
+
+        def load_ts(n):
+            a, q = 1 - n // 4, n % 4
+            r0 = 32 * q + 4 * (1 - a)
+            nc.sync.dma_start(ts[r0:r0 + 4, :], tab_scales[a, 4 * q:4 * q + 4, :].bitcast(I32))
+
         nc.sync.dma_start(tw[1][:], tab_words[1].rearrange("p t i -> p (t i)").bitcast(I32))
-        for a in (1, 0):
-            for q in range(4):
-                r0 = 32 * q + 4 * (1 - a)
-                if (a, q) == (0, 3):
-                    nc.sync.dma_start(keys[:], offs)
-                eng = nc.sync if (a, q) == (0, 3) else nc.scalar
-                eng.dma_start(ts[r0:r0 + 4, :], tab_scales[a, 4 * q:4 * q + 4, :].bitcast(I32))
+        for n in range(4):
+            load_ts(n)
+        nc.sync.dma_start(keys[:], offs)
         nc.sync.dma_start(wc[0][:], wcut[:, 0:512].rearrange("(p j) c -> p j c", j=4))
+        for n in range(4, 8):
+            load_ts(n)
         nc.sync.dma_start(cyls[:], offs2)
         nc.sync.dma_start(wc[1][:], wcut[:, 512:1024].rearrange("(p j) c -> p j c", j=4))
         nc.sync.dma_start(tw[0][:], tab_words[0].rearrange("p t i -> p (t i)").bitcast(I32))
@@ -132,15 +135,16 @@ def tile_list_keying_risk_scores_kernel(tc, tab_words, tab_scales, offs, offs2, 
                     for u in range(2):
                         i = 2 * pair + u
                         nc.vector.scalar_tensor_tensor(res[:, u, :], acc[:, u, :], tl[:, i:i + 1], up[:, u, :], ALU.min, ALU.subtract, reverse1=True)
-                nc.sync.dma_start(out[256 * pair:256 * pair + 256, n].rearrange("(u p) j -> p u j", p=P), res[:])
+                        nc.sync.dma_start(out[128 * i:128 * i + 128, n], res[:, u, :])
+                if pair < shared:
+                    nc.sync.dma_start(out[256 * pair:256 * pair + 256, n].rearrange("(u p) j -> p u j", p=P), res[:])
 
         nc.vector.tensor_copy(wsp[:].rearrange("p (b t o i) -> p b o t i", b=2, t=4, i=16),
                               ws[:].bitcast(U8).rearrange("p (b o i t) -> p b o t i", b=2, t=4, i=16))
         nc.vector.tensor_copy(wwp[:].bitcast(U16).rearrange("p (b t o i) -> p b o t i", b=2, t=4, i=8),
                               ww[:].bitcast(U16).rearrange("p (b o i t) -> p b o t i", b=2, t=4, i=8))
         gather_words(kw1[:], 1, keys, 0, 1024)
-        gather_scales(ks, keys, 0, 512)
-        gather_scales(ks, keys, 512, 1024)
+        gather_scales(ks, keys, 0, 1024)
         gather_scales(cs, cyls, 0, 512)
         cast(0)
         quant_w(0)
@@ -149,21 +153,21 @@ def tile_list_keying_risk_scores_kernel(tc, tab_words, tab_scales, offs, offs2, 
         gather_words(kw0[0][:, 0:256], 0, keys, 0, 256)
         quant_w(1)
         gather_words(kw0[0][:, 256:512], 0, keys, 256, 512)
+        kw0[1] = keep.tile([P, 512], U32, name="kw0b", align_bytes=64)
+        gather_words(kw0[1][:], 0, keys, 512, 1024)
         cw[1] = keep.tile([P, S2], U32, name="cw1", tag="wcb1", align_bytes=64)
         gather_words(cw[1][:], 1, cyls, 0, 512)
         cw[0] = keep.tile([P, S2], U32, name="cw0", align_bytes=64)
         gather_words(cw[0][:], 0, cyls, 0, 512)
-        stage1(0, 0)
-        stage1(1, 0)
-        kw0[1] = keep.tile([P, 512], U32, name="kw0b", tag="hb1_0", align_bytes=64)
-        gather_words(kw0[1][:], 0, keys, 512, 1024)
-        stage1(0, 256)
-        stage1(1, 256)
+        stage1(0,0)
+        stage1(1,0)
+        stage1(0,256)
+        stage1(1,256)
+        stage1(0,512)
         stage2(0, 0)
-        stage1(0, 512)
-        stage1(1, 512)
+        stage1(1,512)
         stage2(256, 0)
-        stage1(0, 768)
-        stage1(1, 768)
+        stage1(0,768)
+        stage1(1,768)
         stage2(512, 0)
         stage2(768, 0)

@@ -38,28 +38,29 @@ def tile_list_keying_risk_scores_kernel(tc, tab_words, tab_scales, offs, offs2, 
         nc.vector.memset(ws[:], 0)
         nc.vector.memset(ts[:], 0)
         nc.sync.dma_start(ww[:], wway_words[0].bitcast(I32))
-        for q in range(4):
-            nc.sync.dma_start(ws[32 * q:32 * q + 4, :], wway_scales[0, 4 * q:4 * q + 4, :].bitcast(I32))
+        for r in range(4):
+            nc.sync.dma_start(ws[r:P:32, :], wway_scales[0, r:16:4, :].bitcast(I32))
 
         def load_ts(n):
-            a, q = 1 - n // 4, n % 4
-            r0 = 32 * q + 4 * (1 - a)
-            nc.sync.dma_start(ts[r0:r0 + 4, :], tab_scales[a, 4 * q:4 * q + 4, :].bitcast(I32))
+            a, r = 1 - n // 4, n % 4
+            nc.sync.dma_start(ts[4 * (1 - a) + r:P:32, :], tab_scales[a, r:16:4, :].bitcast(I32))
 
+        load_ts(0)
+        load_ts(1)
         nc.sync.dma_start(tw[1][:], tab_words[1].rearrange("p t i -> p (t i)").bitcast(I32))
-        for n in range(4):
-            load_ts(n)
         nc.sync.dma_start(keys[:], offs)
-        nc.sync.dma_start(wc[0][:], wcut[:, 0:512].rearrange("(p j) c -> p j c", j=4))
-        for n in range(4, 8):
-            load_ts(n)
         nc.sync.dma_start(cyls[:], offs2)
+        for n in range(2, 6):
+            load_ts(n)
+        nc.sync.dma_start(wc[0][:], wcut[:, 0:512].rearrange("(p j) c -> p j c", j=4))
+        load_ts(6)
+        load_ts(7)
         nc.sync.dma_start(wc[1][:], wcut[:, 512:1024].rearrange("(p j) c -> p j c", j=4))
         nc.sync.dma_start(tw[0][:], tab_words[0].rearrange("p t i -> p (t i)").bitcast(I32))
+        nc.sync.dma_start(bs[0][:], base[:, 0:512].rearrange("(i p) j -> p i j", p=P))
         with nc.allow_non_contiguous_dma(reason="one tolerance a partition"):
             nc.sync.dma_start(tl[:], tol.rearrange("(i p) -> p i", p=P))
-        for h in range(2):
-            nc.sync.dma_start(bs[h][:], base[:, 512 * h:512 * h + 512].rearrange("(i p) j -> p i j", p=P))
+        nc.sync.dma_start(bs[1][:], base[:, 512:1024].rearrange("(i p) j -> p i j", p=P))
 
         kw1 = keep.tile([P, S], U32, name="kw1", align_bytes=64)
         kw0 = {}
@@ -144,6 +145,8 @@ def tile_list_keying_risk_scores_kernel(tc, tab_words, tab_scales, offs, offs2, 
         nc.vector.tensor_copy(wwp[:].bitcast(U16).rearrange("p (b t o i) -> p b o t i", b=2, t=4, i=8),
                               ww[:].bitcast(U16).rearrange("p (b o i t) -> p b o t i", b=2, t=4, i=8))
         gather_words(kw1[:], 1, keys, 0, 1024)
+        cw[1] = keep.tile([P, S2], U32, name="cw1", align_bytes=64)
+        gather_words(cw[1][:], 1, cyls, 0, 512)
         gather_scales(ks, keys, 0, 1024)
         gather_scales(cs, cyls, 0, 512)
         cast(0)
@@ -155,8 +158,6 @@ def tile_list_keying_risk_scores_kernel(tc, tab_words, tab_scales, offs, offs2, 
         gather_words(kw0[0][:, 256:512], 0, keys, 256, 512)
         kw0[1] = keep.tile([P, 512], U32, name="kw0b", align_bytes=64)
         gather_words(kw0[1][:], 0, keys, 512, 1024)
-        cw[1] = keep.tile([P, S2], U32, name="cw1", tag="wcb1", align_bytes=64)
-        gather_words(cw[1][:], 1, cyls, 0, 512)
         cw[0] = keep.tile([P, S2], U32, name="cw0", align_bytes=64)
         gather_words(cw[0][:], 0, cyls, 0, 512)
         stage1(0,0)

from contextlib import ExitStack

import concourse.mybir as mybir

F32 = mybir.dt.float32
BF16 = mybir.dt.bfloat16
I32 = mybir.dt.int32
U32 = mybir.dt.uint32
U16 = mybir.dt.uint16
U8 = mybir.dt.uint8
E4M3 = mybir.dt.float8_e4m3fn_x4
E2M1 = mybir.dt.float4_e2m1fn_x4
ALU = mybir.AluOpType
ACT = mybir.ActivationFunctionType

P = 128
K, T, S, S2 = 1024, 2048, 1024, 512
FLOPS = 2 * K * K * S + 2 * K * S2 * S


def tile_list_keying_risk_scores_kernel(tc, tab_words, tab_scales, offs, offs2, wcut, wway_words, wway_scales, base, tol, out):
    nc = tc.nc
    with ExitStack() as ctx:
        keep = ctx.enter_context(tc.tile_pool(name="keep", bufs=1))
        ring = ctx.enter_context(tc.tile_pool(name="ring", bufs=4))
        ps = ctx.enter_context(tc.psum_pool(name="ps", bufs=8))

        keys = keep.tile([P, S // 16], U16, name="keys")
        cyls = keep.tile([P, S2 // 16], U16, name="cyls")
        ts = keep.tile([P, T // 4], I32, name="ts", align_bytes=64)
        ws = keep.tile([P, K // 4], I32, name="ws", align_bytes=64)
        ww = keep.tile([P, K // 2], I32, name="ww", align_bytes=64)
        tw = [keep.tile([P, T], I32, name="tw%d" % a, align_bytes=64) for a in range(2)]
        wc = [keep.tile([P, 4, 512], F32, name="wc%d" % b, align_bytes=64) for b in range(2)]
        bs = [keep.tile([P, 4, 512], F32, name="bs%d" % h, align_bytes=64) for h in range(2)]
        tl = keep.tile([P, 4], F32, name="tl")

        nc.vector.memset(ws[:], 0)
        nc.vector.memset(ts[:], 0)
        nc.sync.dma_start(ww[:], wway_words[0].bitcast(I32))
        for r in range(4):
            nc.sync.dma_start(ws[r:P:32, :], wway_scales[0, r:16:4, :].bitcast(I32))

        def load_ts(n):
            a, r = 1 - n // 4, n % 4
            nc.sync.dma_start(ts[4 * (1 - a) + r:P:32, :], tab_scales[a, r:16:4, :].bitcast(I32))

        load_ts(0)
        load_ts(1)
        nc.sync.dma_start(tw[1][:], tab_words[1].rearrange("p t i -> p (t i)").bitcast(I32))
        nc.sync.dma_start(keys[:], offs)
        nc.sync.dma_start(cyls[:], offs2)
        for n in range(2, 6):
            load_ts(n)
        nc.sync.dma_start(wc[0][:], wcut[:, 0:512].rearrange("(p j) c -> p j c", j=4))
        load_ts(6)
        load_ts(7)
        nc.sync.dma_start(wc[1][:], wcut[:, 512:1024].rearrange("(p j) c -> p j c", j=4))
        nc.sync.dma_start(tw[0][:], tab_words[0].rearrange("p t i -> p (t i)").bitcast(I32))
        nc.sync.dma_start(bs[0][:], base[:, 0:512].rearrange("(i p) j -> p i j", p=P))
        with nc.allow_non_contiguous_dma(reason="one tolerance a partition"):
            nc.sync.dma_start(tl[:], tol.rearrange("(i p) -> p i", p=P))
        nc.sync.dma_start(bs[1][:], base[:, 512:1024].rearrange("(i p) j -> p i j", p=P))

        kw1 = keep.tile([P, S], U32, name="kw1", align_bytes=64)
        kw0 = {}
        ks = keep.tile([P, S], U8, name="ks", align_bytes=64)
        cw = {}
        cs = keep.tile([P, S2], U8, name="cs", align_bytes=64)
        wwp = keep.tile([P, 2 * K], U8, name="wwp", align_bytes=64)
        wsp = keep.tile([P, K], U8, name="wsp", align_bytes=64)
        wcb = [keep.tile([P, 2048], BF16, name="wcb%d" % b, tag="wcb%d" % b, align_bytes=64) for b in range(2)]
        wcq = [keep.tile([P, 512], U32, name="wcq%d" % b, align_bytes=64) for b in range(2)]
        wcs = [keep.tile([P, 512], U8, name="wcs%d" % b, align_bytes=64) for b in range(2)]
        hq = [keep.tile([P, S], U32, name="hq%d" % b, align_bytes=64) for b in range(2)]
        hs = [keep.tile([P, S], U8, name="hs%d" % b, align_bytes=64) for b in range(2)]

        def gather_scales(dst, lst, j0, j1):
            nc.vector.tensor_copy(dst[:, j0:j1], ts[:].bitcast(U8).indirect(lst[:, j0 // 16:j1 // 16]))

        def gather_words(dst, a, lst, j0, j1):
            nc.vector.tensor_copy(dst, tw[a][:].bitcast(U32).indirect(lst[:, j0 // 16:j1 // 16]))

        def cast(b):
            nc.scalar.activation(
                wcb[b][:].rearrange("p (t m j) -> p m t j", t=4, j=4),
                wc[b][:].rearrange("p j (m t) -> p m t j", t=4), ACT.Copy)

        def quant_w(b):
            nc.vector.quantize_mx(wcq[b][:].bitcast(E4M3), wcs[b][:], wcb[b][:])

        def stage1(b, j0):
            hb = keep.tile([P, 256, 4], BF16, name="hb", tag="hb%d_%d" % (b, j0), align_bytes=64)
            for c in range(2):
                n = slice(j0 + 128 * c, j0 + 128 * c + 128)
                acc = ps.tile([P, 4, 128], F32, name="acc")
                for t in range(4):
                    c0 = 512 * b + 128 * t
                    nc.tensor.matmul_mx(acc[:, t, :], lhsT=wwp[:, 2 * c0:2 * c0 + 256].bitcast(E2M1), lhsT_scale=wsp[:, c0:c0 + 128],
                                        rhs=kw1[:, n].bitcast(E4M3), rhs_scale=ks[:, n], start=(t == 0), stop=False)
                for t in range(4):
                    nc.tensor.matmul_mx(acc[:, t, :], lhsT=wcq[b][:, 128 * t:128 * t + 128].bitcast(E4M3), lhsT_scale=wcs[b][:, 128 * t:128 * t + 128],
                                        rhs=kw0[j0 // 512][:, n.start % 512:n.start % 512 + 128].bitcast(E4M3), rhs_scale=ks[4:P, n], start=False, stop=(t == 3))
                nc.scalar.activation(hb[:, 128 * c:128 * c + 128, :], acc[:].rearrange("p t n -> p n t"), ACT.Abs)
            nc.vector.quantize_mx(hq[b][:, j0:j0 + 256].bitcast(E4M3), hs[b][:, j0:j0 + 256], hb[:].rearrange("p n t -> p (n t)"))

        def stage2(j0, shared):
            h, o = divmod(j0, 512)
            n = slice(j0, j0 + 256)
            tiles = []
            for pair in range(2):
                acc = ps.tile([P, 2, 256], F32, name="acc")
                for u in range(2):
                    m = slice(256 * pair + 128 * u, 256 * pair + 128 * u + 128)
                    nc.tensor.matmul_mx(acc[:, u, :], lhsT=cw[0][:, m].bitcast(E4M3), lhsT_scale=cs[4:P, m],
                                        rhs=hq[0][:, n].bitcast(E4M3), rhs_scale=hs[0][:, n], start=True, stop=False)
                    nc.tensor.matmul_mx(acc[:, u, :], lhsT=cw[1][:, m].bitcast(E4M3), lhsT_scale=cs[:, m],
                                        rhs=hq[1][:, n].bitcast(E4M3), rhs_scale=hs[1][:, n], start=False, stop=True)
                up = ring.tile([P, 2, 256], F32, name="up")
                if pair < shared:
                    nc.vector.tensor_tensor(up[:], bs[h][:, 2 * pair:2 * pair + 2, o:o + 256], acc[:], ALU.subtract)
                else:
                    nc.vector.tensor_tensor(up[:], acc[:], bs[h][:, 2 * pair:2 * pair + 2, o:o + 256], ALU.max)
                tiles.append((pair, acc, up))
            for pair, acc, up in tiles:
                res = ring.tile([P, 2, 256], F32, name="res", bufs=8)
                if pair < shared:
                    over = ring.tile([P, 2, 256], F32, name="over")
                    under = ring.tile([P, 2, 256], F32, name="under")
                    for u in range(2):
                        i = 2 * pair + u
                        nc.scalar.activation(over[:, u, :], acc[:, u, :], ACT.Relu, bias=tl[:, i:i + 1])
                    nc.scalar.activation(under[:], up[:], ACT.Relu)
                    nc.gpsimd.tensor_tensor(res[:], over[:], under[:], ALU.add)
                else:
                    for u in range(2):
                        i = 2 * pair + u
                        nc.vector.scalar_tensor_tensor(res[:, u, :], acc[:, u, :], tl[:, i:i + 1], up[:, u, :], ALU.min, ALU.subtract, reverse1=True)
                        nc.sync.dma_start(out[128 * i:128 * i + 128, n], res[:, u, :])
                if pair < shared:
                    nc.sync.dma_start(out[256 * pair:256 * pair + 256, n].rearrange("(u p) j -> p u j", p=P), res[:])

        nc.vector.tensor_copy(wsp[:].rearrange("p (b t o i) -> p b o t i", b=2, t=4, i=16),
                              ws[:].bitcast(U8).rearrange("p (b o i t) -> p b o t i", b=2, t=4, i=16))
        nc.vector.tensor_copy(wwp[:].bitcast(U16).rearrange("p (b t o i) -> p b o t i", b=2, t=4, i=8),
                              ww[:].bitcast(U16).rearrange("p (b o i t) -> p b o t i", b=2, t=4, i=8))
        gather_words(kw1[:], 1, keys, 0, 1024)
        cw[1] = keep.tile([P, S2], U32, name="cw1", align_bytes=64)
        gather_words(cw[1][:], 1, cyls, 0, 512)
        gather_scales(ks, keys, 0, 1024)
        gather_scales(cs, cyls, 0, 512)
        cast(0)
        quant_w(0)
        cast(1)
        kw0[0] = keep.tile([P, 512], U32, name="kw0a", align_bytes=64)
        gather_words(kw0[0][:, 0:256], 0, keys, 0, 256)
        quant_w(1)
        gather_words(kw0[0][:, 256:512], 0, keys, 256, 512)
        kw0[1] = keep.tile([P, 512], U32, name="kw0b", align_bytes=64)
        gather_words(kw0[1][:], 0, keys, 512, 1024)
        cw[0] = keep.tile([P, S2], U32, name="cw0", align_bytes=64)
        gather_words(cw[0][:], 0, cyls, 0, 512)
        stage1(0,0)
        stage1(1,0)
        stage1(0,256)
        stage1(1,256)
        stage1(0,512)
        stage2(0, 0)
        stage1(1,512)
        stage2(256, 0)
        stage1(0,768)
        stage1(1,768)
        stage2(512, 0)
        stage2(768, 0)
